import numpy as np
import ml_dtypes

BF16 = ml_dtypes.bfloat16


def bf(x):
    return np.asarray(x, np.float32).astype(BF16)


def f32(x):
    return np.asarray(x, np.float32)


def f64(x):
    return np.asarray(x).astype(np.float64)


def striped(idx):
    return np.concatenate([l.reshape(-1, 16).T for l in idx])


def rows(idx, k):
    return np.tile(np.repeat(idx, 16, axis=0), (k // (16 * 8), 1))


def look(tab, idx):
    return np.take_along_axis(f64(tab), rows(idx, len(tab)), axis=1)


K, S, D, V, N, M = 256, 2048, 2, 1024, 2048, 128


def setup_inputs():
    return {"tab": f32(np.random.standard_normal((K, S))), "x0": f32(np.random.standard_normal((K, V))), "w": bf(np.random.standard_normal((K, M)) / np.sqrt(K)), "offs": striped(np.stack([np.random.permutation(S)[:N] for _ in range(8)]))}


def reference(tab, x0, w, offs):
    idx = np.stack([g.T.reshape(-1) for g in np.split(offs, 8)])
    x = f64(x0)
    for d in range(D):
        x = np.minimum(x, look(tab, idx[:, d * V:(d + 1) * V]))
    y = f64(w).T @ x
    return y

@@ -1,0 +1,55 @@
+import concourse.mybir as mybir
+
+F32, BF16, U16 = mybir.dt.float32, mybir.dt.bfloat16, mybir.dt.uint16
+MIN = mybir.AluOpType.min
+
+P = 128
+PIECE = 512
+GROUP = 16
+
+FLOPS = 2 * 256 * 128 * 1024
+
+
+def tile_lookup_pool_min_none_kernel(tc, tab, x0, w, offs, out):
+    nc = tc.nc
+    rows, slots = tab.shape
+    centres = x0.shape[1]
+    features = w.shape[1]
+    blocks, pieces = rows // P, centres // PIECE
+
+    with (
+        tc.tile_pool(name="held", bufs=1) as held,
+        tc.psum_pool(name="psum", bufs=1) as psum,
+    ):
+        offsets = held.tile([P, offs.shape[1]], U16, name="offsets")
+        weights = held.tile([P, blocks, features], BF16, name="weights")
+        tables = [held.tile([P, slots], F32, name=f"table{b}") for b in range(blocks)]
+        own = [held.tile([P, centres], F32, name=f"own{b}") for b in range(blocks)]
+        banks = [psum.tile([P, PIECE], F32, name=f"bank{c}") for c in range(pieces)]
+
+        nc.sync.dma_start(offsets[:], offs)
+        for b in range(blocks):
+            nc.sync.dma_start(tables[b][:], tab[b * P:(b + 1) * P, :])
+            nc.sync.dma_start(own[b][:], x0[b * P:(b + 1) * P, :])
+        nc.sync.dma_start(weights[:], w.rearrange("(b p) m -> p b m", p=P))
+
+        def neighbours(b, first_entry):
+            start = first_entry // GROUP
+            return tables[b][:].indirect(offsets[:, start:start + PIECE // GROUP])
+
+        for b in range(blocks):
+            for c in range(pieces):
+                first_min = held.tile([P, PIECE], F32, name=f"first_min{b}_{c}")
+                pooled = held.tile([P, PIECE], F32, name=f"pooled{b}_{c}")
+                rounded = held.tile([P, PIECE], BF16, name=f"rounded{b}_{c}")
+                nc.vector.tensor_tensor(first_min[:], neighbours(b, c * PIECE),
+                                        own[b][:, c * PIECE:(c + 1) * PIECE], MIN)
+                nc.vector.tensor_tensor(pooled[:], neighbours(b, centres + c * PIECE), first_min[:], MIN)
+                nc.scalar.copy(rounded[:], pooled[:])
+                nc.tensor.matmul(banks[c][:], weights[:, b, :], rounded[:],
+                                 start=(b == 0), stop=(b == blocks - 1))
+
+        for c in range(pieces):
+            result = held.tile([P, PIECE], F32, name=f"result{c}")
+            nc.scalar.copy(result[:], banks[c][:])
+            nc.sync.dma_start(out[:, c * PIECE:(c + 1) * PIECE], result[:])

@@ -6,6 +6,7 @@ MIN = mybir.AluOpType.min
 P = 128
 PIECE = 512
 GROUP = 16
+PARTS = 4
 
 FLOPS = 2 * 256 * 128 * 1024
 
@@ -17,6 +18,9 @@ def tile_lookup_pool_min_none_kernel(tc, tab, x0, w, offs, out):
     features = w.shape[1]
     blocks, pieces = rows // P, centres // PIECE
 
+    part = PIECE // PARTS
+    half = PIECE // 2
+
     with (
         tc.tile_pool(name="held", bufs=1) as held,
         tc.psum_pool(name="psum", bufs=1) as psum,
@@ -24,32 +28,42 @@ def tile_lookup_pool_min_none_kernel(tc, tab, x0, w, offs, out):
         offsets = held.tile([P, offs.shape[1]], U16, name="offsets")
         weights = held.tile([P, blocks, features], BF16, name="weights")
         tables = [held.tile([P, slots], F32, name=f"table{b}") for b in range(blocks)]
-        own = [held.tile([P, centres], F32, name=f"own{b}") for b in range(blocks)]
-        banks = [psum.tile([P, PIECE], F32, name=f"bank{c}") for c in range(pieces)]
+        own = [[held.tile([P, PIECE], F32, name=f"own{b}_{c}") for c in range(pieces)] for b in range(blocks)]
+        banks = [psum.tile([P, part], F32, name=f"bank{q}") for q in range(centres // part)]
 
-        nc.sync.dma_start(offsets[:], offs)
         for b in range(blocks):
             nc.sync.dma_start(tables[b][:], tab[b * P:(b + 1) * P, :])
-            nc.sync.dma_start(own[b][:], x0[b * P:(b + 1) * P, :])
-        nc.sync.dma_start(weights[:], w.rearrange("(b p) m -> p b m", p=P))
+            for c in range(pieces):
+                nc.sync.dma_start(own[b][c][:], x0[b * P:(b + 1) * P, c * PIECE:(c + 1) * PIECE])
+                if b == 0 and c == 0:
+                    nc.sync.dma_start(offsets[:], offs)
+            if b == 0:
+                nc.sync.dma_start(weights[:], w.rearrange("(b p) m -> p b m", p=P))
 
         def neighbours(b, first_entry):
             start = first_entry // GROUP
             return tables[b][:].indirect(offsets[:, start:start + PIECE // GROUP])
 
         for b in range(blocks):
+            first_min = [held.tile([P, PIECE], F32, name=f"first_min{b}_{c}") for c in range(pieces)]
             for c in range(pieces):
-                first_min = held.tile([P, PIECE], F32, name=f"first_min{b}_{c}")
+                nc.vector.tensor_tensor(first_min[c][:], neighbours(b, c * PIECE), own[b][c][:], MIN)
+            for c in range(pieces):
                 pooled = held.tile([P, PIECE], F32, name=f"pooled{b}_{c}")
                 rounded = held.tile([P, PIECE], BF16, name=f"rounded{b}_{c}")
-                nc.vector.tensor_tensor(first_min[:], neighbours(b, c * PIECE),
-                                        own[b][:, c * PIECE:(c + 1) * PIECE], MIN)
-                nc.vector.tensor_tensor(pooled[:], neighbours(b, centres + c * PIECE), first_min[:], MIN)
-                nc.scalar.copy(rounded[:], pooled[:])
-                nc.tensor.matmul(banks[c][:], weights[:, b, :], rounded[:],
-                                 start=(b == 0), stop=(b == blocks - 1))
+                nc.vector.tensor_tensor(pooled[:], neighbours(b, centres + c * PIECE), first_min[c][:], MIN)
+                last_lookup = b == blocks - 1 and c == pieces - 1
+                cast = nc.vector.tensor_copy if last_lookup else nc.scalar.copy
+                for q in range(PARTS):
+                    columns = slice(q * part, (q + 1) * part)
+                    cast(rounded[:, columns], pooled[:, columns])
+                    nc.tensor.matmul(banks[PARTS * c + q][:], weights[:, b, :], rounded[:, columns],
+                                     start=(b == 0), stop=(b == blocks - 1))
 
-        for c in range(pieces):
-            result = held.tile([P, PIECE], F32, name=f"result{c}")
-            nc.scalar.copy(result[:], banks[c][:])
-            nc.sync.dma_start(out[:, c * PIECE:(c + 1) * PIECE], result[:])
+        halves = centres // half
+        for h in range(halves):
+            result = held.tile([P, half], F32, name=f"result{h}")
+            copy = nc.vector.tensor_copy if h == halves - 1 else nc.scalar.copy
+            for q in range(PARTS // 2):
+                copy(result[:, q * part:(q + 1) * part], banks[h * PARTS // 2 + q][:])
+            nc.sync.dma_start(out[:, h * half:(h + 1) * half], result[:])

@@ -34,8 +34,10 @@ def tile_lookup_pool_min_none_kernel(tc, tab, x0, w, offs, out):
         for b in range(blocks):
             nc.sync.dma_start(tables[b][:], tab[b * P:(b + 1) * P, :])
             for c in range(pieces):
-                nc.sync.dma_start(own[b][c][:], x0[b * P:(b + 1) * P, c * PIECE:(c + 1) * PIECE])
-                if b == 0 and c == 0:
+                first_piece = b == 0 and c == 0
+                queue = nc.scalar if first_piece else nc.sync
+                queue.dma_start(own[b][c][:], x0[b * P:(b + 1) * P, c * PIECE:(c + 1) * PIECE])
+                if first_piece:
                     nc.sync.dma_start(offsets[:], offs)
             if b == 0:
                 nc.sync.dma_start(weights[:], w.rearrange("(b p) m -> p b m", p=P))
@@ -66,4 +68,5 @@ def tile_lookup_pool_min_none_kernel(tc, tab, x0, w, offs, out):
             copy = nc.vector.tensor_copy if h == halves - 1 else nc.scalar.copy
             for q in range(PARTS // 2):
                 copy(result[:, q * part:(q + 1) * part], banks[h * PARTS // 2 + q][:])
-            nc.sync.dma_start(out[:, h * half:(h + 1) * half], result[:])
+            queue = nc.scalar if h == halves - 2 else nc.sync
+            queue.dma_start(out[:, h * half:(h + 1) * half], result[:])

import concourse.mybir as mybir

F32, BF16, U16 = mybir.dt.float32, mybir.dt.bfloat16, mybir.dt.uint16
MIN = mybir.AluOpType.min

P = 128
PIECE = 512
GROUP = 16
PARTS = 4

FLOPS = 2 * 256 * 128 * 1024


def tile_lookup_pool_min_none_kernel(tc, tab, x0, w, offs, out):
    nc = tc.nc
    rows, slots = tab.shape
    centres = x0.shape[1]
    features = w.shape[1]
    blocks, pieces = rows // P, centres // PIECE

    part = PIECE // PARTS
    half = PIECE // 2

    with (
        tc.tile_pool(name="held", bufs=1) as held,
        tc.psum_pool(name="psum", bufs=1) as psum,
    ):
        offsets = held.tile([P, offs.shape[1]], U16, name="offsets")
        weights = held.tile([P, blocks, features], BF16, name="weights")
        tables = [held.tile([P, slots], F32, name=f"table{b}") for b in range(blocks)]
        own = [[held.tile([P, PIECE], F32, name=f"own{b}_{c}") for c in range(pieces)] for b in range(blocks)]
        banks = [psum.tile([P, part], F32, name=f"bank{q}") for q in range(centres // part)]

        for b in range(blocks):
            nc.sync.dma_start(tables[b][:], tab[b * P:(b + 1) * P, :])
            for c in range(pieces):
                first_piece = b == 0 and c == 0
                queue = nc.scalar if first_piece else nc.sync
                queue.dma_start(own[b][c][:], x0[b * P:(b + 1) * P, c * PIECE:(c + 1) * PIECE])
                if first_piece:
                    nc.sync.dma_start(offsets[:], offs)
            if b == 0:
                nc.sync.dma_start(weights[:], w.rearrange("(b p) m -> p b m", p=P))

        def neighbours(b, first_entry):
            start = first_entry // GROUP
            return tables[b][:].indirect(offsets[:, start:start + PIECE // GROUP])

        for b in range(blocks):
            first_min = [held.tile([P, PIECE], F32, name=f"first_min{b}_{c}") for c in range(pieces)]
            for c in range(pieces):
                nc.vector.tensor_tensor(first_min[c][:], neighbours(b, c * PIECE), own[b][c][:], MIN)
            for c in range(pieces):
                pooled = held.tile([P, PIECE], F32, name=f"pooled{b}_{c}")
                rounded = held.tile([P, PIECE], BF16, name=f"rounded{b}_{c}")
                nc.vector.tensor_tensor(pooled[:], neighbours(b, centres + c * PIECE), first_min[c][:], MIN)
                last_lookup = b == blocks - 1 and c == pieces - 1
                cast = nc.vector.tensor_copy if last_lookup else nc.scalar.copy
                for q in range(PARTS):
                    columns = slice(q * part, (q + 1) * part)
                    cast(rounded[:, columns], pooled[:, columns])
                    nc.tensor.matmul(banks[PARTS * c + q][:], weights[:, b, :], rounded[:, columns],
                                     start=(b == 0), stop=(b == blocks - 1))

        halves = centres // half
        for h in range(halves):
            result = held.tile([P, half], F32, name=f"result{h}")
            copy = nc.vector.tensor_copy if h == halves - 1 else nc.scalar.copy
            for q in range(PARTS // 2):
                copy(result[:, q * part:(q + 1) * part], banks[h * PARTS // 2 + q][:])
            queue = nc.scalar if h == halves - 2 else nc.sync
            queue.dma_start(out[:, h * half:(h + 1) * half], result[:])
